import numpy as np, ml_dtypes
CORES = [8,80,112,136,208,240,264,336,368,392,464,496]
N = 12
W, KW, DIL = 512, 5, 1
H = (KW // 2) * DIL
def setup_inputs(rng):
    return {"x": rng.standard_normal((N, 128, W), dtype=np.float32).astype(ml_dtypes.bfloat16), "w": rng.standard_normal((N, 128, KW * 128), dtype=np.float32).astype(ml_dtypes.bfloat16)}
def setup_inputs_big(rng):
    d = setup_inputs(rng)
    for k in ("x", "w"): d[k] = (d[k].astype(np.float32) * 1024.0).astype(d[k].dtype)
    return d
def setup_inputs_small(rng):
    d = setup_inputs(rng)
    for k in ("x", "w"): d[k] = (d[k].astype(np.float32) * (1 / 1024.0)).astype(d[k].dtype)
    return d
def reference(x, w):
    X, W_ = x.astype(np.float64), w.astype(np.float64)
    g = np.concatenate(list(X), axis=1)
    p = np.concatenate([g[:, -H:], g, g[:, :H]], axis=1)
    y = np.zeros((N, 128, W))
    for r in range(N):
        for i in range(KW):
            y[r] += W_[r][:, 128 * i:128 * i + 128].T @ p[:, W * r + i * DIL:W * r + i * DIL + W]
    return {"y": y.astype(ml_dtypes.bfloat16 if x.dtype != np.float64 else np.float64)}

from concourse.bass import DstId, RemoteDMATransfer

P = 128
W = 512
KW = 5
H = 2
MID = 258
E_FWD = 4

SCRATCH = {
    "xs": ("sbuf", [P, W + 2 * H], "bfloat16"),
    "ws": ("sbuf", [P, KW * P], "bfloat16"),
    "ya": ("sbuf", [P, MID - H], "bfloat16"),
    "yb": ("sbuf", [P, W - H - MID], "bfloat16"),
    "yl": ("sbuf", [P, H], "bfloat16"),
    "yr": ("sbuf", [P, H], "bfloat16"),
    "hl": ("dram", [P, H], "bfloat16"),
    "hr": ("dram", [P, H], "bfloat16"),
    "hb": ("dram", [P, H], "bfloat16"),
    "pa": ("psum", [P, 512], "float32"),
    "pb": ("psum", [P, 512], "float32"),
    "pl": ("psum", [P, 512], "float32"),
    "pr": ("psum", [P, 512], "float32"),
}
SEMAPHORES = ["hl", "hr", "x", "w", "relay", "sent", "left", "right",
              "ma", "mb", "ml", "mr", "ca", "cb", "cl", "cr", "sa", "sb", "sl", "sr"]

_CACHE = {}


def _engines(mask, n, top=False, skip=0):
    bits = [b for b in range(mask.bit_length()) if (mask >> b) & 1]
    if top:
        bits = bits[::-1]
    m = 0
    for b in bits[skip:skip + n]:
        m |= 1 << b
    return m


def _plan(T, topo):
    if "plan" in _CACHE:
        return _CACHE["plan"]
    cores = list(T.cores)
    n = len(cores)
    world = (max(topo.host(c) for c in cores) + 1) * topo.CORES_PER_HOST
    sends, helpers, direct = {}, {}, {r: [] for r in range(n)}
    for r, src in enumerate(cores):
        sends[r] = []
        for stage, step, side in (("hl", -1, "right"), ("hr", 1, "left")):
            q = (r + step) % n
            dst = cores[q]
            via = None
            if topo.may_write(src, dst):
                direct[q].append(side)
            else:
                cand = [c for c in range(world)
                        if topo.host(c) == topo.host(src) and topo.chip(c) == topo.chip(src) and c != src
                        and c not in cores and c not in helpers
                        and topo.may_write(src, c) and topo.may_write(c, dst)]
                cand.sort(key=lambda c: (topo.die(c) != topo.die(src), c))
                via = cand[0]
                helpers[via] = (dst, side)
            sends[r].append((stage, dst, via, side))
    _CACHE["plan"] = (sends, helpers, direct)
    return _CACHE["plan"]


def _landing(T, side):
    return T.xs[:, 0:H] if side == "left" else T.xs[:, W + H:W + 2 * H]


def rank_program(g, core, T, topo):
    sends, helpers, direct = _plan(T, topo)
    sem = T.sem

    if core in helpers:
        dst, side = helpers[core]
        rid, pid = topo.addr(dst, core)
        g.wait_ge(sem.relay, 1)
        g.remote_dma(out_ap=_landing(T, side), in_ap=T.hb[:, :], remote_sem=sem[side], local_sem=sem.sent,
                     pid=pid, routing_id=rid, dma_engine_mask=_engines(topo.mask(core, dst), E_FWD))
        g.wait_ge(sem.sent, E_FWD)
        return

    rank = T.rank_of(core)
    if rank is None:
        return

    g.sync.dma_start(T.hl[:, :], T.x[:, 0:H]).then_inc(sem.hl, 16)
    g.scalar.dma_start(T.hr[:, :], T.x[:, W - H:W]).then_inc(sem.hr, 16)
    g.sync.dma_start(T.xs[:, H:W + H], T.x[:, :]).then_inc(sem.x, 16)
    g.scalar.dma_start(T.ws[:, :], T.w[:, :]).then_inc(sem.w, 16)

    relays = [s for s in sends[rank] if s[2] is not None]
    straight = [s for s in sends[rank] if s[2] is None]
    sent = 0
    for stage, dst, via, side in relays:
        g.wait_ge(sem[stage], 16)
    if len(relays) == 1:
        stage, dst, via, side = relays[0]
        rid, pid = topo.addr(via, core)
        g.remote_dma(out_ap=T.hb[:, :], in_ap=T[stage][:, :], remote_sem=sem.relay, local_sem=sem.sent,
                     pid=pid, routing_id=rid, dma_engine_mask=_engines(topo.mask(core, via), 1, top=True))
        sent += 1
    elif relays:
        trs = []
        for k, (stage, dst, via, side) in enumerate(relays):
            rid, pid = topo.addr(via, core)
            trs.append(RemoteDMATransfer(dst_ids=[DstId(rid=rid, pnc=pid)],
                                         dma_engine_mask=_engines(topo.mask(core, via), 1, top=True, skip=k),
                                         remote_sem=sem.relay, src=T[stage][:, :], dst=T.hb[:, :]))
            sent += 1
        g.remote_dma_fused(trs, local_sem=sem.sent)
    for stage, dst, via, side in straight:
        rid, pid = topo.addr(dst, core)
        g.wait_ge(sem[stage], 16)
        g.remote_dma(out_ap=_landing(T, side), in_ap=T[stage][:, :], remote_sem=sem[side], local_sem=sem.sent,
                     pid=pid, routing_id=rid, dma_engine_mask=_engines(topo.mask(core, dst), E_FWD))
        sent += E_FWD
    g.wait_ge(sem.sent, sent)

    order = sorted(("left", "right"), key=lambda s: s not in direct[rank])

    def tap(i):
        return T.ws[:, P * i:P * (i + 1)]

    te = g.tensor
    te.wait_ge(sem.x, 16)
    te.wait_ge(sem.w, 16)
    for out, lo, hi, done in ((T.pa, H, MID, sem.ma), (T.pb, MID, W - H, sem.mb)):
        for i in range(KW):
            mm = te.matmul(out[:, 0:hi - lo], tap(i), T.xs[:, lo + i:hi + i], start=(i == 0), stop=(i == KW - 1))
        mm.then_inc(done, 1)
    edge = {"left": (T.pl, 0, [2, 3, 4], [1, 0], sem.ml), "right": (T.pr, W - H, [2, 1, 0], [3, 4], sem.mr)}
    for s in order:
        out, c0, own, late, done = edge[s]
        for k, i in enumerate(own):
            te.matmul(out[:, 0:H], tap(i), T.xs[:, c0 + i:c0 + i + H], start=(k == 0), stop=False)
    for s in order:
        out, c0, own, late, done = edge[s]
        te.wait_ge(sem[s], E_FWD)
        for k, i in enumerate(late):
            mm = te.matmul(out[:, 0:H], tap(i), T.xs[:, c0 + i:c0 + i + H], start=False, stop=(k == len(late) - 1))
        mm.then_inc(done, 1)

    ve = g.vector
    ve.wait_ge(sem.ma, 1)
    ve.tensor_copy(T.ya[:, :], T.pa[:, 0:MID - H]).then_inc(sem.ca, 1)
    ve.wait_ge(sem.mb, 1)
    ve.tensor_copy(T.yb[:, :], T.pb[:, 0:W - H - MID]).then_inc(sem.cb, 1)
    for s in order:
        if s == "left":
            ve.wait_ge(sem.ml, 1)
            ve.tensor_copy(T.yl[:, :], T.pl[:, 0:H]).then_inc(sem.cl, 1)
        else:
            ve.wait_ge(sem.mr, 1)
            ve.tensor_copy(T.yr[:, :], T.pr[:, 0:H]).then_inc(sem.cr, 1)

    g.sync.wait_ge(sem.ca, 1)
    g.sync.dma_start(T.y[:, H:MID], T.ya[:, :]).then_inc(sem.sa, 16)
    g.scalar.wait_ge(sem.cb, 1)
    g.scalar.dma_start(T.y[:, MID:W - H], T.yb[:, :]).then_inc(sem.sb, 16)
    g.sync.wait_ge(sem.cl, 1)
    g.sync.dma_start(T.y[:, 0:H], T.yl[:, :]).then_inc(sem.sl, 16)
    g.scalar.wait_ge(sem.cr, 1)
    g.scalar.dma_start(T.y[:, W - H:W], T.yr[:, :]).then_inc(sem.sr, 16)
    g.sync.wait_ge(sem.sa, 16)
    g.sync.wait_ge(sem.sl, 16)
    g.scalar.wait_ge(sem.sb, 16)
    g.scalar.wait_ge(sem.sr, 16)
